import numpy as np
import ml_dtypes


def mxq(x, axis, fmt="e4m3"):
    dtype, down = {"e4m3": (ml_dtypes.float8_e4m3fn, 7), "e5m2": (ml_dtypes.float8_e5m2, 14)}[fmt]
    v = np.moveaxis(np.asarray(x, np.float32).astype(ml_dtypes.bfloat16).astype(np.float64), axis, -1)
    blocks = v.reshape(v.shape[:-1] + (-1, 32))
    amax = np.abs(blocks).max(-1, keepdims=True)
    byte = np.maximum(np.where(amax > 0, np.frexp(amax)[1] - 1 + 127, 0) - down, 1)
    scale = np.exp2(byte - 127.0)
    codes = (blocks / scale).astype(np.float32).astype(dtype).astype(np.float64)
    return np.moveaxis((codes * scale).reshape(v.shape), -1, axis)


WIDE = False


def mx_kscale(k):
    if not WIDE:
        return np.ones(k)
    levels = np.array([10, -10, 5, -5, 0])
    if k % 512:
        return np.exp2(np.random.permutation(np.resize(levels, k // 32))).repeat(32)
    a = np.empty((k // 512, 16))
    for p in range(k // 512):
        a[p, :8] = np.random.permutation(np.resize(levels, 8))
        for g in range(8):
            far = levels[np.abs(levels - a[p, g]) >= 10]
            a[p, g + 8] = far[np.random.randint(len(far))]
    return np.exp2(a.ravel()).repeat(32)


def f64(x):
    return np.asarray(x).astype(np.float64)


def striped(idx):
    return np.tile(idx.reshape(-1, 16).T, (8, 1)).astype(np.uint16)


def unstriped(offs):
    return offs[:16].T.reshape(-1).astype(np.int64)


E2M1 = np.array([0.0, 0.5, 1.0, 1.5, 2.0, 3.0, 4.0, 6.0, -0.0, -0.5, -1.0, -1.5, -2.0, -3.0, -4.0, -6.0])


def pack_weight(w, fmt):
    k, n = w.shape
    w = f64(np.asarray(w, np.float32).astype(ml_dtypes.bfloat16)).reshape(k // 32, 32, n)
    amax = np.abs(w).max(1)
    if fmt == "e4m3":
        byte = np.frexp(amax)[1] - 1 + 127 - 7
    else:
        mant, ex = np.frexp(amax / 6.0)
        byte = np.where(mant > 0.5, ex, ex - 1) + 127
    byte = np.clip(np.where(amax > 0, byte, 1), 1, 254)
    scaled = (w * np.exp2(127.0 - byte)[:, None, :]).reshape(k, n).astype(np.float32)
    by_word = np.ascontiguousarray(scaled.reshape(k // 512, 128, 4, n).transpose(0, 1, 3, 2))
    if fmt == "e4m3":
        words = by_word.astype(ml_dtypes.float8_e4m3fn).view(np.uint8)
    else:
        c = by_word.astype(ml_dtypes.float4_e2m1fn).view(np.uint8) & 0xF
        words = (c[..., 0::2] | (c[..., 1::2] << 4)).reshape(k // 512, 128, 2 * n)
    return np.ascontiguousarray(words), np.ascontiguousarray(byte.astype(np.uint8).reshape(k // 512, 16, n))


def unpack_weight(words, scales, fmt):
    g, _, n = scales.shape
    words = np.ascontiguousarray(words).reshape(g, 128, n, -1)
    if fmt == "e4m3":
        vals = words.view(ml_dtypes.float8_e4m3fn).astype(np.float64)
    else:
        nib = np.empty((g, 128, n, 4), np.uint8)
        nib[..., 0::2] = words & 0xF
        nib[..., 1::2] = words >> 4
        vals = E2M1[nib]
    vals = vals * np.repeat(np.exp2(scales.astype(np.float64) - 127.0), 8, axis=1)[..., None]
    return vals.transpose(0, 1, 3, 2).reshape(g * 512, n)


def silu(v):
    return v / (1.0 + np.exp(-np.maximum(v, -700.0)))


K, T, E, C, H, N = 512, 1024, 4, 256, 512, 256


def by_expert(wq, xq):
    return np.concatenate([wq[e].T @ xq[:, e * C:(e + 1) * C] for e in range(E)], axis=1)


def setup_inputs():
    n = np.random.standard_normal
    s = mx_kscale(K)[:, None]
    u = mx_kscale(H)
    w1 = [pack_weight(m, "e2m1") for m in n((E, K, H)) / np.sqrt(K) / s[None]]
    w3 = [pack_weight(m, "e2m1") for m in n((E, K, H)) / np.sqrt(K) / s[None] * u[None, None, :]]
    w2 = [pack_weight(m, "e2m1") for m in n((E, H, N)) / np.sqrt(H) / u[None, :, None]]
    return {
        "xT": (n((K, T)) * s).astype(np.float32),
        "w1_words": np.stack([m[0] for m in w1]),
        "w1_scales": np.stack([m[1] for m in w1]),
        "w3_words": np.stack([m[0] for m in w3]),
        "w3_scales": np.stack([m[1] for m in w3]),
        "w2_words": np.stack([m[0] for m in w2]),
        "w2_scales": np.stack([m[1] for m in w2]),
        "gate": np.tile(np.random.uniform(0.2, 1.0, E * C), (N, 1)).astype(np.float32),
        "offs": striped(np.random.permutation(T)[:E * C]),
        "dst": striped(np.random.permutation(T)[:E * C]),
    }


def reference(xT, w1_words, w1_scales, w3_words, w3_scales, w2_words, w2_scales, gate, offs, dst):
    idx = unstriped(offs)
    w1 = np.stack([unpack_weight(w1_words[e], w1_scales[e], "e2m1") for e in range(E)])
    w3 = np.stack([unpack_weight(w3_words[e], w3_scales[e], "e2m1") for e in range(E)])
    w2 = np.stack([unpack_weight(w2_words[e], w2_scales[e], "e2m1") for e in range(E)])
    xq = mxq(f64(xT)[:, idx], 0, "e4m3")
    h = silu(by_expert(w1, xq))
    h = h * by_expert(w3, xq)
    y = by_expert(w2, mxq(h, 0, "e4m3"))
    out = np.zeros((N, T))
    out[:, unstriped(dst)] = f64(gate) * y
    return out

@@ -1,0 +1,196 @@
+from contextlib import ExitStack
+
+import concourse.mybir as mybir
+from concourse.masks import make_identity
+
+K, T, E, C, H, N = 512, 1024, 4, 256, 512, 256
+FLOPS = 2 * E * C * (K * H + K * H + H * N)
+
+P = 128
+BLK = 128
+NBLK = E * C // BLK
+CHUNKS = (256, 256, 256, 256)
+
+F32 = mybir.dt.float32
+BF16 = mybir.dt.bfloat16
+I32 = mybir.dt.int32
+U32 = mybir.dt.uint32
+U16 = mybir.dt.uint16
+U8 = mybir.dt.uint8
+FP8 = mybir.dt.float8_e4m3fn_x4
+FP4 = mybir.dt.float4_e2m1fn_x4
+ACT = mybir.ActivationFunctionType
+MULT = mybir.AluOpType.mult
+
+
+def tile_moe_two_glu_silu_kernel(
+    tc, xT, w1_words, w1_scales, w3_words, w3_scales, w2_words, w2_scales, gate, offs, dst, out
+):
+    nc = tc.nc
+    with ExitStack() as ctx:
+        keep = ctx.enter_context(tc.tile_pool(name="keep", bufs=1))
+        work = ctx.enter_context(tc.tile_pool(name="work", bufs=3))
+        psum = ctx.enter_context(tc.psum_pool(name="psum", bufs=2))
+
+        offs_sb = keep.tile([P, E * C // 16], U16, name="offs_sb")
+        dst_sb = keep.tile([P, E * C // 16], U16, name="dst_sb")
+        w1s = keep.tile([P, E * H], U8, name="w1s", align_bytes=256)
+        w3s = keep.tile([P, E * H], U8, name="w3s", align_bytes=256)
+        w2s = keep.tile([P, E * N], U8, name="w2s", align_bytes=256)
+        xsc = keep.tile([P, T], U8, name="xsc", align_bytes=256)
+        xcd = keep.tile([P, T], U32, name="xcd", align_bytes=256)
+        ident = keep.tile([P, P], F32, name="ident", align_bytes=256)
+        gate_sb = keep.tile([P, 2, E * C], F32, name="gate_sb", align_bytes=256)
+        win = [keep.tile([P, T], F32, name=f"win{m}", align_bytes=256) for m in range(2)]
+
+        nc.vector.memset(w1s[:].bitcast(I32), 0)
+        nc.vector.memset(w3s[:].bitcast(I32), 0)
+        nc.vector.memset(w2s[:].bitcast(I32), 0)
+        nc.gpsimd.memset(xsc[:], 0)
+        make_identity(nc, ident[:])
+        warm = keep.tile([P, 1], F32, name="warm")
+        nc.vector.memset(warm[:], 0.0)
+        nc.scalar.activation(warm[:], warm[:], ACT.Silu)
+
+        def load_scales(plane, src, width):
+            for q in range(4):
+                nc.sync.dma_start(
+                    out=plane[32 * q : 32 * q + 4, :].rearrange("r (e i) -> r e i", e=E).bitcast(I32),
+                    in_=src[:, 0, 4 * q : 4 * q + 4, :].rearrange("e r i -> r e i").bitcast(I32),
+                )
+
+        xin = xT.rearrange("(p j) t -> p j t", j=4)
+        xf = []
+
+        def load_x(i):
+            c0 = sum(CHUNKS[:i])
+            t = keep.tile([P, 4, CHUNKS[i]], F32, name=f"xf{i}", align_bytes=256)
+            nc.sync.dma_start(out=t[:], in_=xin[:, :, c0 : c0 + CHUNKS[i]])
+            xf.append(t)
+
+        wt = {}
+
+        def load_w(key, src, e):
+            width = src.shape[3]
+            t = keep.tile([P, width], U8, name=f"{key}{e}", align_bytes=256)
+            nc.sync.dma_start(out=t[:].bitcast(I32), in_=src[e, 0].bitcast(I32))
+            wt[key, e] = t
+
+        nc.sync.dma_start(offs_sb[:], offs)
+        load_x(0)
+        load_x(1)
+        load_scales(w1s, w1_scales, H)
+        for i in range(2, len(CHUNKS)):
+            load_x(i)
+        load_scales(w3s, w3_scales, H)
+        load_w("w1", w1_words, 0)
+        load_w("w3", w3_words, 0)
+        load_w("w1", w1_words, 1)
+        load_w("w3", w3_words, 1)
+        load_scales(w2s, w2_scales, N)
+        load_w("w2", w2_words, 0)
+        nc.sync.dma_start(dst_sb[:], dst)
+        gsrc = gate.rearrange("(m p) j -> p m j", m=2)
+        nc.sync.dma_start(out=gate_sb[:], in_=gsrc)
+        load_w("w1", w1_words, 2)
+        load_w("w3", w3_words, 2)
+        load_w("w2", w2_words, 1)
+        load_w("w1", w1_words, 3)
+        load_w("w3", w3_words, 3)
+        load_w("w2", w2_words, 2)
+        load_w("w2", w2_words, 3)
+
+        c0 = 0
+        for i, w in enumerate(CHUNKS):
+            xb = keep.tile([P, w, 4], BF16, name=f"xb{i}", align_bytes=256)
+            nc.vector.tensor_copy(out=xb[:], in_=xf[i][:].rearrange("p j w -> p w j"))
+            nc.vector.quantize_mx(
+                out=xcd[:, c0 : c0 + w].bitcast(FP8), scales=xsc[:, c0 : c0 + w], in_=xb[:].rearrange("p w j -> p (w j)")
+            )
+            c0 += w
+
+        codes, scales = {}, {}
+
+        def gather(e):
+            cols = slice(e * C // 16, (e + 1) * C // 16)
+            cd = keep.tile([P, C], U32, name=f"cd{e}", align_bytes=256)
+            sc = keep.tile([P, C], U8, name=f"sc{e}", align_bytes=256)
+            nc.vector.tensor_copy(cd[:], xcd[:].indirect(offs_sb[:, cols]))
+            nc.vector.tensor_copy(sc[:], xsc[:].indirect(offs_sb[:, cols]))
+            codes[e], scales[e] = cd, sc
+
+        st = {}
+
+        def project(b):
+            e, s = b // 2, slice(b % 2 * BLK, b % 2 * BLK + BLK)
+            pa = psum.tile([P, H], F32, name="pa")
+            pb = psum.tile([P, H], F32, name="pb")
+            for ps, key, pl in ((pa, "w1", w1s), (pb, "w3", w3s)):
+                nc.tensor.matmul_mx(
+                    out=ps[:],
+                    lhsT=codes[e][:, s].bitcast(FP8),
+                    lhsT_scale=scales[e][:, s],
+                    rhs=wt[key, e][:].bitcast(FP4),
+                    rhs_scale=pl[:, e * H : (e + 1) * H],
+                    start=True,
+                    stop=True,
+                )
+            sil = work.tile([P, H], F32, name="sil", align_bytes=256)
+            nc.scalar.activation(sil[:], pa[:], ACT.Silu)
+            st["sil", b], st["pb", b] = sil, pb
+
+        def product(b):
+            h = work.tile([P, H], BF16, name="h", align_bytes=256)
+            nc.vector.tensor_tensor(h[:], st["sil", b][:], st["pb", b][:], MULT)
+            words = h[:].bitcast(F32)
+            pt = psum.tile([P, 2, BLK], F32, name="pt")
+            for u in range(2):
+                nc.tensor.transpose(pt[:, u, :], words[:, u : H // 2 : 2], ident[:])
+            hg = work.tile([P, BLK, 4], BF16, name="hg", align_bytes=256)
+            nc.scalar.copy(hg[:].rearrange("p s t -> p (s t)").bitcast(F32).rearrange("p (s u) -> p s u", u=2), pt[:].rearrange("p u s -> p s u"))
+            st["hg", b] = hg
+
+        def down(b):
+            e, half = b // 2, b % 2
+            hc = work.tile([P, BLK], U32, name="hc", align_bytes=256)
+            hs = work.tile([P, BLK], U8, name="hs", align_bytes=256)
+            nc.vector.quantize_mx(out=hc[:].bitcast(FP8), scales=hs[:], in_=st["hg", b][:].rearrange("p s t -> p (s t)"))
+            if half == 0:
+                st["py", e] = psum.tile([P, 2, C], F32, name="py")
+            py = st["py", e]
+            for m in range(2):
+                nc.tensor.matmul_mx(
+                    out=py[:, m, half * BLK : half * BLK + BLK],
+                    lhsT=wt["w2", e][:, m * 256 : m * 256 + 256].bitcast(FP4),
+                    lhsT_scale=w2s[:, e * N + m * P : e * N + m * P + P],
+                    rhs=hc[:].bitcast(FP8),
+                    rhs_scale=hs[:],
+                    start=True,
+                    stop=True,
+                )
+
+        def place(e):
+            py = st["py", e]
+            ys = work.tile([P, 2, C], F32, name="ys", align_bytes=256)
+            cols = slice(e * C // 16, (e + 1) * C // 16)
+            nc.vector.tensor_tensor(ys[:], py[:], gate_sb[:, :, e * C : (e + 1) * C], MULT)
+            for m in range(2):
+                nc.vector.tensor_copy(win[m][:].indirect(dst_sb[:, cols]), ys[:, m, :])
+
+        gather(0)
+        gather(1)
+        for s in range(NBLK + 3):
+            if s < NBLK:
+                project(s)
+            if s == 1:
+                gather(2)
+            if s == 2:
+                gather(3)
+            if 1 <= s <= NBLK:
+                product(s - 1)
+            if 2 <= s <= NBLK + 1:
+                down(s - 2)
+            if s >= 4 and s % 2 == 0:
+                place((s - 4) // 2)
+        for m in range(2):
+            nc.sync.dma_start(out=out[m * P : (m + 1) * P, :], in_=win[m][:])

@@ -9,7 +9,7 @@ FLOPS = 2 * E * C * (K * H + K * H + H * N)
 P = 128
 BLK = 128
 NBLK = E * C // BLK
-CHUNKS = (256, 256, 256, 256)
+CHUNKS = (512, 256, 256)
 
 F32 = mybir.dt.float32
 BF16 = mybir.dt.bfloat16
@@ -29,8 +29,8 @@ def tile_moe_two_glu_silu_kernel(
     nc = tc.nc
     with ExitStack() as ctx:
         keep = ctx.enter_context(tc.tile_pool(name="keep", bufs=1))
-        work = ctx.enter_context(tc.tile_pool(name="work", bufs=3))
-        psum = ctx.enter_context(tc.psum_pool(name="psum", bufs=2))
+        work = ctx.enter_context(tc.tile_pool(name="work", bufs=8))
+        psum = ctx.enter_context(tc.psum_pool(name="psum", bufs=1))
 
         offs_sb = keep.tile([P, E * C // 16], U16, name="offs_sb")
         dst_sb = keep.tile([P, E * C // 16], U16, name="dst_sb")
@@ -43,95 +43,87 @@ def tile_moe_two_glu_silu_kernel(
         gate_sb = keep.tile([P, 2, E * C], F32, name="gate_sb", align_bytes=256)
         win = [keep.tile([P, T], F32, name=f"win{m}", align_bytes=256) for m in range(2)]
 
-        nc.vector.memset(w1s[:].bitcast(I32), 0)
-        nc.vector.memset(w3s[:].bitcast(I32), 0)
-        nc.vector.memset(w2s[:].bitcast(I32), 0)
-        nc.gpsimd.memset(xsc[:], 0)
-        make_identity(nc, ident[:])
+        for plane in (w1s, w3s, w2s):
+            nc.vector.memset(plane[:].bitcast(I32), 0)
         warm = keep.tile([P, 1], F32, name="warm")
         nc.vector.memset(warm[:], 0.0)
-        nc.scalar.activation(warm[:], warm[:], ACT.Silu)
+        nc.gpsimd.memset(xsc[:], 0)
 
-        def load_scales(plane, src, width):
+        def load_scales(eng, plane, src):
             for q in range(4):
-                nc.sync.dma_start(
+                eng.dma_start(
                     out=plane[32 * q : 32 * q + 4, :].rearrange("r (e i) -> r e i", e=E).bitcast(I32),
                     in_=src[:, 0, 4 * q : 4 * q + 4, :].rearrange("e r i -> r e i").bitcast(I32),
                 )
 
         xin = xT.rearrange("(p j) t -> p j t", j=4)
         xf = []
-
-        def load_x(i):
-            c0 = sum(CHUNKS[:i])
-            t = keep.tile([P, 4, CHUNKS[i]], F32, name=f"xf{i}", align_bytes=256)
-            nc.sync.dma_start(out=t[:], in_=xin[:, :, c0 : c0 + CHUNKS[i]])
+        c0 = 0
+        for i, w in enumerate(CHUNKS):
+            t = keep.tile([P, 4, w], F32, name=f"xf{i}", align_bytes=256)
+            nc.sync.dma_start(out=t[:], in_=xin[:, :, c0 : c0 + w])
             xf.append(t)
+            c0 += w
+        load_scales(nc.scalar, w1s, w1_scales)
+        load_scales(nc.gpsimd, w3s, w3_scales)
+        nc.scalar.activation(warm[:], warm[:], ACT.Silu)
+        make_identity(nc, ident[:])
+        nc.sync.dma_start(offs_sb[:], offs)
 
         wt = {}
 
-        def load_w(key, src, e):
+        def load_w(key, src, e0, n):
             width = src.shape[3]
-            t = keep.tile([P, width], U8, name=f"{key}{e}", align_bytes=256)
-            nc.sync.dma_start(out=t[:].bitcast(I32), in_=src[e, 0].bitcast(I32))
-            wt[key, e] = t
+            t = keep.tile([P, n, width], U8, name=f"{key}_{e0}", align_bytes=256)
+            nc.sync.dma_start(out=t[:].bitcast(I32), in_=src[e0 : e0 + n, 0].rearrange("e p b -> p e b").bitcast(I32))
+            for i in range(n):
+                wt[key, e0 + i] = t[:, i, :]
 
-        nc.sync.dma_start(offs_sb[:], offs)
-        load_x(0)
-        load_x(1)
-        load_scales(w1s, w1_scales, H)
-        for i in range(2, len(CHUNKS)):
-            load_x(i)
-        load_scales(w3s, w3_scales, H)
-        load_w("w1", w1_words, 0)
-        load_w("w3", w3_words, 0)
-        load_w("w1", w1_words, 1)
-        load_w("w3", w3_words, 1)
-        load_scales(w2s, w2_scales, N)
-        load_w("w2", w2_words, 0)
+        load_w("w1", w1_words, 0, 1)
+        load_w("w3", w3_words, 0, 1)
+        load_w("w1", w1_words, 1, 3)
+        load_w("w3", w3_words, 1, 3)
+        load_scales(nc.sync, w2s, w2_scales)
+        load_w("w2", w2_words, 0, 4)
         nc.sync.dma_start(dst_sb[:], dst)
-        gsrc = gate.rearrange("(m p) j -> p m j", m=2)
-        nc.sync.dma_start(out=gate_sb[:], in_=gsrc)
-        load_w("w1", w1_words, 2)
-        load_w("w3", w3_words, 2)
-        load_w("w2", w2_words, 1)
-        load_w("w1", w1_words, 3)
-        load_w("w3", w3_words, 3)
-        load_w("w2", w2_words, 2)
-        load_w("w2", w2_words, 3)
+        nc.sync.dma_start(out=gate_sb[:], in_=gate.rearrange("(m p) j -> p m j", m=2))
 
-        c0 = 0
-        for i, w in enumerate(CHUNKS):
-            xb = keep.tile([P, w, 4], BF16, name=f"xb{i}", align_bytes=256)
-            nc.vector.tensor_copy(out=xb[:], in_=xf[i][:].rearrange("p j w -> p w j"))
+        for i, lo, w, caster in ((0, 0, 256, "s"), (0, 256, 256, "v"), (1, 0, 256, "v"), (2, 0, 128, "s"), (2, 128, 128, "v")):
+            xb = keep.tile([P, w, 4], BF16, name=f"xb{i}_{lo}", align_bytes=256)
+            src = xf[i][:, :, lo : lo + w].rearrange("p j w -> p w j")
+            if caster == "s":
+                nc.scalar.copy(xb[:], src)
+            else:
+                nc.vector.tensor_copy(xb[:], src)
+            c0 = sum(CHUNKS[:i]) + lo
             nc.vector.quantize_mx(
                 out=xcd[:, c0 : c0 + w].bitcast(FP8), scales=xsc[:, c0 : c0 + w], in_=xb[:].rearrange("p w j -> p (w j)")
             )
-            c0 += w
 
         codes, scales = {}, {}
 
-        def gather(e):
-            cols = slice(e * C // 16, (e + 1) * C // 16)
-            cd = keep.tile([P, C], U32, name=f"cd{e}", align_bytes=256)
-            sc = keep.tile([P, C], U8, name=f"sc{e}", align_bytes=256)
+        def gather(b, n):
+            cols = slice(b * BLK // 16, (b + n) * BLK // 16)
+            cd = keep.tile([P, n * BLK], U32, name=f"cd{b}", align_bytes=256)
+            sc = keep.tile([P, n * BLK], U8, name=f"sc{b}", align_bytes=256)
             nc.vector.tensor_copy(cd[:], xcd[:].indirect(offs_sb[:, cols]))
             nc.vector.tensor_copy(sc[:], xsc[:].indirect(offs_sb[:, cols]))
-            codes[e], scales[e] = cd, sc
+            for i in range(n):
+                codes[b + i], scales[b + i] = cd[:, i * BLK : (i + 1) * BLK], sc[:, i * BLK : (i + 1) * BLK]
 
         st = {}
 
         def project(b):
-            e, s = b // 2, slice(b % 2 * BLK, b % 2 * BLK + BLK)
-            pa = psum.tile([P, H], F32, name="pa")
-            pb = psum.tile([P, H], F32, name="pb")
-            for ps, key, pl in ((pa, "w1", w1s), (pb, "w3", w3s)):
+            e = b // 2
+            pa = psum.tile([P, H], F32, name="pa", bufs=2)
+            pb = psum.tile([P, H], F32, name="pb", bufs=3)
+            for ps, key, plane in ((pa, "w1", w1s), (pb, "w3", w3s)):
                 nc.tensor.matmul_mx(
                     out=ps[:],
-                    lhsT=codes[e][:, s].bitcast(FP8),
-                    lhsT_scale=scales[e][:, s],
-                    rhs=wt[key, e][:].bitcast(FP4),
-                    rhs_scale=pl[:, e * H : (e + 1) * H],
+                    lhsT=codes[b].bitcast(FP8),
+                    lhsT_scale=scales[b],
+                    rhs=wt[key, e].bitcast(FP4),
+                    rhs_scale=plane[:, e * H : (e + 1) * H],
                     start=True,
                     stop=True,
                 )
@@ -151,16 +143,14 @@ def tile_moe_two_glu_silu_kernel(
             st["hg", b] = hg
 
         def down(b):
-            e, half = b // 2, b % 2
+            e = b // 2
             hc = work.tile([P, BLK], U32, name="hc", align_bytes=256)
             hs = work.tile([P, BLK], U8, name="hs", align_bytes=256)
             nc.vector.quantize_mx(out=hc[:].bitcast(FP8), scales=hs[:], in_=st["hg", b][:].rearrange("p s t -> p (s t)"))
-            if half == 0:
-                st["py", e] = psum.tile([P, 2, C], F32, name="py")
-            py = st["py", e]
+            py = psum.tile([P, 2, BLK], F32, name="py", bufs=2)
             for m in range(2):
                 nc.tensor.matmul_mx(
-                    out=py[:, m, half * BLK : half * BLK + BLK],
+                    out=py[:, m, :],
                     lhsT=wt["w2", e][:, m * 256 : m * 256 + 256].bitcast(FP4),
                     lhsT_scale=w2s[:, e * N + m * P : e * N + m * P + P],
                     rhs=hc[:].bitcast(FP8),
@@ -168,29 +158,26 @@ def tile_moe_two_glu_silu_kernel(
                     start=True,
                     stop=True,
                 )
+            ys = work.tile([P, 2, BLK], F32, name="ys", align_bytes=256)
+            nc.scalar.copy(ys[:], py[:])
+            st["ys", b] = ys
 
-        def place(e):
-            py = st["py", e]
-            ys = work.tile([P, 2, C], F32, name="ys", align_bytes=256)
-            cols = slice(e * C // 16, (e + 1) * C // 16)
-            nc.vector.tensor_tensor(ys[:], py[:], gate_sb[:, :, e * C : (e + 1) * C], MULT)
+        def place(b):
+            cols = slice(b * BLK // 16, (b + 1) * BLK // 16)
             for m in range(2):
-                nc.vector.tensor_copy(win[m][:].indirect(dst_sb[:, cols]), ys[:, m, :])
+                nc.vector.tensor_tensor(win[m][:].indirect(dst_sb[:, cols]), st["ys", b][:, m, :], gate_sb[:, m, b * BLK : (b + 1) * BLK], MULT)
 
-        gather(0)
-        gather(1)
+        gathers = {0: ((0, 1), (1, 1)), 1: ((2, 2),), 3: ((4, 2),), 4: ((6, 2),)}
         for s in range(NBLK + 3):
+            for g in gathers.get(s, ()):
+                gather(*g)
             if s < NBLK:
                 project(s)
-            if s == 1:
-                gather(2)
-            if s == 2:
-                gather(3)
             if 1 <= s <= NBLK:
                 product(s - 1)
             if 2 <= s <= NBLK + 1:
                 down(s - 2)
-            if s >= 4 and s % 2 == 0:
-                place((s - 4) // 2)
+            if s >= 3:
+                place(s - 3)
         for m in range(2):
             nc.sync.dma_start(out=out[m * P : (m + 1) * P, :], in_=win[m][:])

@@ -35,7 +35,8 @@ def tile_moe_two_glu_silu_kernel(
         offs_sb = keep.tile([P, E * C // 16], U16, name="offs_sb")
         dst_sb = keep.tile([P, E * C // 16], U16, name="dst_sb")
         w1s = keep.tile([P, E * H], U8, name="w1s", align_bytes=256)
-        w3s = keep.tile([P, E * H], U8, name="w3s", align_bytes=256)
+        w3a = keep.tile([P, H], U8, name="w3a", align_bytes=256)
+        w3b = keep.tile([P, (E - 1) * H], U8, name="w3b", align_bytes=256)
         w2s = keep.tile([P, E * N], U8, name="w2s", align_bytes=256)
         xsc = keep.tile([P, T], U8, name="xsc", align_bytes=256)
         xcd = keep.tile([P, T], U32, name="xcd", align_bytes=256)
@@ -43,17 +44,17 @@ def tile_moe_two_glu_silu_kernel(
         gate_sb = keep.tile([P, 2, E * C], F32, name="gate_sb", align_bytes=256)
         win = [keep.tile([P, T], F32, name=f"win{m}", align_bytes=256) for m in range(2)]
 
-        for plane in (w1s, w3s, w2s):
+        for plane in (w3a, w1s, w3b, w2s):
             nc.vector.memset(plane[:].bitcast(I32), 0)
         warm = keep.tile([P, 1], F32, name="warm")
         nc.vector.memset(warm[:], 0.0)
-        nc.gpsimd.memset(xsc[:], 0)
+        nc.gpsimd.memset(xsc[:].bitcast(I32), 0)
 
-        def load_scales(eng, plane, src):
+        def load_scales(eng, plane, src, e0=0, n=E):
             for q in range(4):
                 eng.dma_start(
-                    out=plane[32 * q : 32 * q + 4, :].rearrange("r (e i) -> r e i", e=E).bitcast(I32),
-                    in_=src[:, 0, 4 * q : 4 * q + 4, :].rearrange("e r i -> r e i").bitcast(I32),
+                    out=plane[32 * q : 32 * q + 4, :].rearrange("r (e i) -> r e i", e=n).bitcast(I32),
+                    in_=src[e0 : e0 + n, 0, 4 * q : 4 * q + 4, :].rearrange("e r i -> r e i").bitcast(I32),
                 )
 
         xin = xT.rearrange("(p j) t -> p j t", j=4)
@@ -64,11 +65,12 @@ def tile_moe_two_glu_silu_kernel(
             nc.sync.dma_start(out=t[:], in_=xin[:, :, c0 : c0 + w])
             xf.append(t)
             c0 += w
-        load_scales(nc.scalar, w1s, w1_scales)
-        load_scales(nc.gpsimd, w3s, w3_scales)
+        nc.sync.dma_start(offs_sb[:], offs)
+        load_scales(nc.sync, w1s, w1_scales)
+        load_scales(nc.gpsimd, w3a, w3_scales, 0, 1)
         nc.scalar.activation(warm[:], warm[:], ACT.Silu)
         make_identity(nc, ident[:])
-        nc.sync.dma_start(offs_sb[:], offs)
+        load_scales(nc.gpsimd, w3b, w3_scales, 1, 3)
 
         wt = {}
 
@@ -117,13 +119,14 @@ def tile_moe_two_glu_silu_kernel(
             e = b // 2
             pa = psum.tile([P, H], F32, name="pa", bufs=2)
             pb = psum.tile([P, H], F32, name="pb", bufs=3)
-            for ps, key, plane in ((pa, "w1", w1s), (pb, "w3", w3s)):
+            w3s = w3a[:] if e == 0 else w3b[:, (e - 1) * H : e * H]
+            for ps, key, plane in ((pa, "w1", w1s[:, e * H : (e + 1) * H]), (pb, "w3", w3s)):
                 nc.tensor.matmul_mx(
                     out=ps[:],
                     lhsT=codes[b].bitcast(FP8),
                     lhsT_scale=scales[b],
                     rhs=wt[key, e].bitcast(FP4),
-                    rhs_scale=plane[:, e * H : (e + 1) * H],
+                    rhs_scale=plane,
                     start=True,
                     stop=True,
                 )
@@ -162,10 +165,9 @@ def tile_moe_two_glu_silu_kernel(
             nc.scalar.copy(ys[:], py[:])
             st["ys", b] = ys
 
-        def place(b):
+        def place(b, m):
             cols = slice(b * BLK // 16, (b + 1) * BLK // 16)
-            for m in range(2):
-                nc.vector.tensor_tensor(win[m][:].indirect(dst_sb[:, cols]), st["ys", b][:, m, :], gate_sb[:, m, b * BLK : (b + 1) * BLK], MULT)
+            nc.vector.tensor_tensor(win[m][:].indirect(dst_sb[:, cols]), st["ys", b][:, m, :], gate_sb[:, m, b * BLK : (b + 1) * BLK], MULT)
 
         gathers = {0: ((0, 1), (1, 1)), 1: ((2, 2),), 3: ((4, 2),), 4: ((6, 2),)}
         for s in range(NBLK + 3):
@@ -177,7 +179,11 @@ def tile_moe_two_glu_silu_kernel(
                 product(s - 1)
             if 2 <= s <= NBLK + 1:
                 down(s - 2)
-            if s >= 3:
-                place(s - 3)
+            if 3 <= s < NBLK + 1:
+                place(s - 3, 0)
+                place(s - 3, 1)
+        for m in range(2):
+            for b in (NBLK - 2, NBLK - 1):
+                place(b, m)
         for m in range(2):
             nc.sync.dma_start(out=out[m * P : (m + 1) * P, :], in_=win[m][:])

from contextlib import ExitStack

import concourse.mybir as mybir
from concourse.masks import make_identity

K, T, E, C, H, N = 512, 1024, 4, 256, 512, 256
FLOPS = 2 * E * C * (K * H + K * H + H * N)

P = 128
BLK = 128
NBLK = E * C // BLK
CHUNKS = (512, 256, 256)

F32 = mybir.dt.float32
BF16 = mybir.dt.bfloat16
I32 = mybir.dt.int32
U32 = mybir.dt.uint32
U16 = mybir.dt.uint16
U8 = mybir.dt.uint8
FP8 = mybir.dt.float8_e4m3fn_x4
FP4 = mybir.dt.float4_e2m1fn_x4
ACT = mybir.ActivationFunctionType
MULT = mybir.AluOpType.mult


def tile_moe_two_glu_silu_kernel(
    tc, xT, w1_words, w1_scales, w3_words, w3_scales, w2_words, w2_scales, gate, offs, dst, out
):
    nc = tc.nc
    with ExitStack() as ctx:
        keep = ctx.enter_context(tc.tile_pool(name="keep", bufs=1))
        work = ctx.enter_context(tc.tile_pool(name="work", bufs=8))
        psum = ctx.enter_context(tc.psum_pool(name="psum", bufs=1))

        offs_sb = keep.tile([P, E * C // 16], U16, name="offs_sb")
        dst_sb = keep.tile([P, E * C // 16], U16, name="dst_sb")
        w1s = keep.tile([P, E * H], U8, name="w1s", align_bytes=256)
        w3a = keep.tile([P, H], U8, name="w3a", align_bytes=256)
        w3b = keep.tile([P, (E - 1) * H], U8, name="w3b", align_bytes=256)
        w2s = keep.tile([P, E * N], U8, name="w2s", align_bytes=256)
        xsc = keep.tile([P, T], U8, name="xsc", align_bytes=256)
        xcd = keep.tile([P, T], U32, name="xcd", align_bytes=256)
        ident = keep.tile([P, P], F32, name="ident", align_bytes=256)
        gate_sb = keep.tile([P, 2, E * C], F32, name="gate_sb", align_bytes=256)
        win = [keep.tile([P, T], F32, name=f"win{m}", align_bytes=256) for m in range(2)]

        for plane in (w3a, w1s, w3b, w2s):
            nc.vector.memset(plane[:].bitcast(I32), 0)
        warm = keep.tile([P, 1], F32, name="warm")
        nc.vector.memset(warm[:], 0.0)
        nc.gpsimd.memset(xsc[:].bitcast(I32), 0)

        def load_scales(eng, plane, src, e0=0, n=E):
            for q in range(4):
                eng.dma_start(
                    out=plane[32 * q : 32 * q + 4, :].rearrange("r (e i) -> r e i", e=n).bitcast(I32),
                    in_=src[e0 : e0 + n, 0, 4 * q : 4 * q + 4, :].rearrange("e r i -> r e i").bitcast(I32),
                )

        xin = xT.rearrange("(p j) t -> p j t", j=4)
        xf = []
        c0 = 0
        for i, w in enumerate(CHUNKS):
            t = keep.tile([P, 4, w], F32, name=f"xf{i}", align_bytes=256)
            nc.sync.dma_start(out=t[:], in_=xin[:, :, c0 : c0 + w])
            xf.append(t)
            c0 += w
        nc.sync.dma_start(offs_sb[:], offs)
        load_scales(nc.sync, w1s, w1_scales)
        load_scales(nc.gpsimd, w3a, w3_scales, 0, 1)
        nc.scalar.activation(warm[:], warm[:], ACT.Silu)
        make_identity(nc, ident[:])
        load_scales(nc.gpsimd, w3b, w3_scales, 1, 3)

        wt = {}

        def load_w(key, src, e0, n):
            width = src.shape[3]
            t = keep.tile([P, n, width], U8, name=f"{key}_{e0}", align_bytes=256)
            nc.sync.dma_start(out=t[:].bitcast(I32), in_=src[e0 : e0 + n, 0].rearrange("e p b -> p e b").bitcast(I32))
            for i in range(n):
                wt[key, e0 + i] = t[:, i, :]

        load_w("w1", w1_words, 0, 1)
        load_w("w3", w3_words, 0, 1)
        load_w("w1", w1_words, 1, 3)
        load_w("w3", w3_words, 1, 3)
        load_scales(nc.sync, w2s, w2_scales)
        load_w("w2", w2_words, 0, 4)
        nc.sync.dma_start(dst_sb[:], dst)
        nc.sync.dma_start(out=gate_sb[:], in_=gate.rearrange("(m p) j -> p m j", m=2))

        for i, lo, w, caster in ((0, 0, 256, "s"), (0, 256, 256, "v"), (1, 0, 256, "v"), (2, 0, 128, "s"), (2, 128, 128, "v")):
            xb = keep.tile([P, w, 4], BF16, name=f"xb{i}_{lo}", align_bytes=256)
            src = xf[i][:, :, lo : lo + w].rearrange("p j w -> p w j")
            if caster == "s":
                nc.scalar.copy(xb[:], src)
            else:
                nc.vector.tensor_copy(xb[:], src)
            c0 = sum(CHUNKS[:i]) + lo
            nc.vector.quantize_mx(
                out=xcd[:, c0 : c0 + w].bitcast(FP8), scales=xsc[:, c0 : c0 + w], in_=xb[:].rearrange("p w j -> p (w j)")
            )

        codes, scales = {}, {}

        def gather(b, n):
            cols = slice(b * BLK // 16, (b + n) * BLK // 16)
            cd = keep.tile([P, n * BLK], U32, name=f"cd{b}", align_bytes=256)
            sc = keep.tile([P, n * BLK], U8, name=f"sc{b}", align_bytes=256)
            nc.vector.tensor_copy(cd[:], xcd[:].indirect(offs_sb[:, cols]))
            nc.vector.tensor_copy(sc[:], xsc[:].indirect(offs_sb[:, cols]))
            for i in range(n):
                codes[b + i], scales[b + i] = cd[:, i * BLK : (i + 1) * BLK], sc[:, i * BLK : (i + 1) * BLK]

        st = {}

        def project(b):
            e = b // 2
            pa = psum.tile([P, H], F32, name="pa", bufs=2)
            pb = psum.tile([P, H], F32, name="pb", bufs=3)
            w3s = w3a[:] if e == 0 else w3b[:, (e - 1) * H : e * H]
            for ps, key, plane in ((pa, "w1", w1s[:, e * H : (e + 1) * H]), (pb, "w3", w3s)):
                nc.tensor.matmul_mx(
                    out=ps[:],
                    lhsT=codes[b].bitcast(FP8),
                    lhsT_scale=scales[b],
                    rhs=wt[key, e].bitcast(FP4),
                    rhs_scale=plane,
                    start=True,
                    stop=True,
                )
            sil = work.tile([P, H], F32, name="sil", align_bytes=256)
            nc.scalar.activation(sil[:], pa[:], ACT.Silu)
            st["sil", b], st["pb", b] = sil, pb

        def product(b):
            h = work.tile([P, H], BF16, name="h", align_bytes=256)
            nc.vector.tensor_tensor(h[:], st["sil", b][:], st["pb", b][:], MULT)
            words = h[:].bitcast(F32)
            pt = psum.tile([P, 2, BLK], F32, name="pt")
            for u in range(2):
                nc.tensor.transpose(pt[:, u, :], words[:, u : H // 2 : 2], ident[:])
            hg = work.tile([P, BLK, 4], BF16, name="hg", align_bytes=256)
            nc.scalar.copy(hg[:].rearrange("p s t -> p (s t)").bitcast(F32).rearrange("p (s u) -> p s u", u=2), pt[:].rearrange("p u s -> p s u"))
            st["hg", b] = hg

        def down(b):
            e = b // 2
            hc = work.tile([P, BLK], U32, name="hc", align_bytes=256)
            hs = work.tile([P, BLK], U8, name="hs", align_bytes=256)
            nc.vector.quantize_mx(out=hc[:].bitcast(FP8), scales=hs[:], in_=st["hg", b][:].rearrange("p s t -> p (s t)"))
            py = psum.tile([P, 2, BLK], F32, name="py", bufs=2)
            for m in range(2):
                nc.tensor.matmul_mx(
                    out=py[:, m, :],
                    lhsT=wt["w2", e][:, m * 256 : m * 256 + 256].bitcast(FP4),
                    lhsT_scale=w2s[:, e * N + m * P : e * N + m * P + P],
                    rhs=hc[:].bitcast(FP8),
                    rhs_scale=hs[:],
                    start=True,
                    stop=True,
                )
            ys = work.tile([P, 2, BLK], F32, name="ys", align_bytes=256)
            nc.scalar.copy(ys[:], py[:])
            st["ys", b] = ys

        def place(b, m):
            cols = slice(b * BLK // 16, (b + 1) * BLK // 16)
            nc.vector.tensor_tensor(win[m][:].indirect(dst_sb[:, cols]), st["ys", b][:, m, :], gate_sb[:, m, b * BLK : (b + 1) * BLK], MULT)

        gathers = {0: ((0, 1), (1, 1)), 1: ((2, 2),), 3: ((4, 2),), 4: ((6, 2),)}
        for s in range(NBLK + 3):
            for g in gathers.get(s, ()):
                gather(*g)
            if s < NBLK:
                project(s)
            if 1 <= s <= NBLK:
                product(s - 1)
            if 2 <= s <= NBLK + 1:
                down(s - 2)
            if 3 <= s < NBLK + 1:
                place(s - 3, 0)
                place(s - 3, 1)
        for m in range(2):
            for b in (NBLK - 2, NBLK - 1):
                place(b, m)
        for m in range(2):
            nc.sync.dma_start(out=out[m * P : (m + 1) * P, :], in_=win[m][:])
